import numpy as np
import ml_dtypes


def mxq(x, axis, fmt="e4m3"):
    dtype, down = {"e4m3": (ml_dtypes.float8_e4m3fn, 7), "e5m2": (ml_dtypes.float8_e5m2, 14)}[fmt]
    v = np.moveaxis(np.asarray(x, np.float32).astype(ml_dtypes.bfloat16).astype(np.float64), axis, -1)
    blocks = v.reshape(v.shape[:-1] + (-1, 32))
    amax = np.abs(blocks).max(-1, keepdims=True)
    byte = np.maximum(np.where(amax > 0, np.frexp(amax)[1] - 1 + 127, 0) - down, 1)
    scale = np.exp2(byte - 127.0)
    codes = (blocks / scale).astype(np.float32).astype(dtype).astype(np.float64)
    return np.moveaxis((codes * scale).reshape(v.shape), -1, axis)


WIDE = False


def mx_kscale(k):
    if not WIDE:
        return np.ones(k)
    levels = np.array([10, -10, 5, -5, 0])
    if k % 512:
        return np.exp2(np.random.permutation(np.resize(levels, k // 32))).repeat(32)
    a = np.empty((k // 512, 16))
    for p in range(k // 512):
        a[p, :8] = np.random.permutation(np.resize(levels, 8))
        for g in range(8):
            far = levels[np.abs(levels - a[p, g]) >= 10]
            a[p, g + 8] = far[np.random.randint(len(far))]
    return np.exp2(a.ravel()).repeat(32)


def f64(x):
    return np.asarray(x).astype(np.float64)


def striped8(idx):
    return np.asarray(idx).reshape(8, -1, 16).transpose(0, 2, 1).reshape(128, -1).astype(np.uint16)


def unstriped8(offs):
    return offs.reshape(8, 16, -1).transpose(0, 2, 1).reshape(8, -1).astype(np.int64)


def pick8(x, idx, run):
    r = np.arange(len(x))
    return x[r[:, None], idx[r % (8 * run) // run]]


E2M1 = np.array([0.0, 0.5, 1.0, 1.5, 2.0, 3.0, 4.0, 6.0, -0.0, -0.5, -1.0, -1.5, -2.0, -3.0, -4.0, -6.0])


def pack_weight(w, fmt):
    k, n = w.shape
    w = f64(np.asarray(w, np.float32).astype(ml_dtypes.bfloat16)).reshape(k // 32, 32, n)
    amax = np.abs(w).max(1)
    if fmt == "e4m3":
        byte = np.frexp(amax)[1] - 1 + 127 - 7
    else:
        mant, ex = np.frexp(amax / 6.0)
        byte = np.where(mant > 0.5, ex, ex - 1) + 127
    byte = np.clip(np.where(amax > 0, byte, 1), 1, 254)
    scaled = (w * np.exp2(127.0 - byte)[:, None, :]).reshape(k, n).astype(np.float32)
    by_word = np.ascontiguousarray(scaled.reshape(k // 512, 128, 4, n).transpose(0, 1, 3, 2))
    if fmt == "e4m3":
        words = by_word.astype(ml_dtypes.float8_e4m3fn).view(np.uint8)
    else:
        c = by_word.astype(ml_dtypes.float4_e2m1fn).view(np.uint8) & 0xF
        words = (c[..., 0::2] | (c[..., 1::2] << 4)).reshape(k // 512, 128, 2 * n)
    return np.ascontiguousarray(words), np.ascontiguousarray(byte.astype(np.uint8).reshape(k // 512, 16, n))


def unpack_weight(words, scales, fmt):
    g, _, n = scales.shape
    words = np.ascontiguousarray(words).reshape(g, 128, n, -1)
    if fmt == "e4m3":
        vals = words.view(ml_dtypes.float8_e4m3fn).astype(np.float64)
    else:
        nib = np.empty((g, 128, n, 4), np.uint8)
        nib[..., 0::2] = words & 0xF
        nib[..., 1::2] = words >> 4
        vals = E2M1[nib]
    vals = vals * np.repeat(np.exp2(scales.astype(np.float64) - 127.0), 8, axis=1)[..., None]
    return vals.transpose(0, 1, 3, 2).reshape(g * 512, n)


D, T, I, Q, G = 512, 1024, 512, 128, 64


def setup_inputs():
    n = np.random.standard_normal
    idx = np.stack([np.random.permutation(T)[:I] for _ in range(8)])
    idx2 = np.stack([np.random.permutation(T)[:I] for _ in range(8)])
    fd = mx_kscale(D)
    keysp = pack_weight(n((D, T)) / fd[:, None], "e2m1")
    return {
        "query": (n((D, Q)) * 0.9 / np.sqrt(D) * fd[:, None]).astype(np.float32),
        "query2": (n((D, Q)) * 0.9 / np.sqrt(D) * fd[:, None]).astype(np.float32),
        "keys_words": keysp[0],
        "keys_scales": keysp[1],
        "mix": (np.random.uniform(0.2, 0.8, (Q, 1))).astype(np.float32),
        "old": (np.random.uniform(0.0, 2.0, (Q, T))).astype(np.float32),
        "fade": (np.random.uniform(0.3, 0.9, (Q, 1))).astype(np.float32),
        "offs": striped8(idx),
        "offs2": striped8(idx2),
    }


def reference(query, query2, keys_words, keys_scales, mix, old, fade, offs, offs2):
    idx = unstriped8(offs)
    idx2 = unstriped8(offs2)
    keysu = unpack_weight(keys_words, keys_scales, "e2m1")
    queryq = mxq(f64(query), 0, "e4m3")
    a = queryq.T @ keysu
    query2q = mxq(f64(query2), 0, "e4m3")
    b = query2q.T @ keysu
    s = pick8(a, idx, 16) * pick8(b, idx2, 16) - pick8(b, idx, 16) * pick8(a, idx2, 16)
    p = np.exp(s - np.max(s, axis=1, keepdims=True))
    r = p / np.sum(p, axis=1, keepdims=True)
    pm = r.reshape(Q, G, I // G).mean(axis=2)
    pr = np.repeat(pm, I // G, axis=1)
    w = r * (1.0 - f64(mix)) + pr * f64(mix)
    ws = w * 256.0
    wf = np.zeros((Q, T))
    wf[np.arange(Q)[:, None], idx[np.arange(Q) % 128 // 16]] = ws
    y = f64(old) * f64(fade) + wf
    return y

@@ -1,0 +1,158 @@
+from contextlib import ExitStack
+
+import concourse.mybir as mybir
+
+D, T, SLOTS, Q, RUN = 512, 1024, 512, 128, 8
+FLOPS = 2 * 2 * D * Q * T
+
+F32 = mybir.dt.float32
+BF16 = mybir.dt.bfloat16
+I32 = mybir.dt.int32
+U32 = mybir.dt.uint32
+U16 = mybir.dt.uint16
+U8 = mybir.dt.uint8
+FP8X4 = mybir.dt.float8_e4m3fn_x4
+FP4X4 = mybir.dt.float4_e2m1fn_x4
+ALU = mybir.AluOpType
+ACT = mybir.ActivationFunctionType
+AX = mybir.AxisListType
+
+P = 128
+PACK = 4
+PIECE = 256
+HALF = SLOTS // 2
+LIST_COLS = SLOTS // 16
+HALF_COLS = LIST_COLS // 2
+STORE = 256
+
+
+def tile_attend_wedge_smoothpage_counts_heads_kernel(
+    tc, query, query2, keys_words, keys_scales, mix, old, fade, offs, offs2, out
+):
+    nc = tc.nc
+    with ExitStack() as ctx:
+        sb = ctx.enter_context(tc.tile_pool(name="sb", bufs=1))
+        ps = ctx.enter_context(tc.psum_pool(name="ps", bufs=1))
+
+        list1 = sb.tile([P, LIST_COLS], U16, name="list1")
+        list2 = sb.tile([P, LIST_COLS], U16, name="list2")
+        q1_raw = sb.tile([P, PACK, Q], F32, name="q1_raw")
+        q2_raw = sb.tile([P, PACK, Q], F32, name="q2_raw")
+        k_words = sb.tile([P, 2 * T], U8, name="k_words", align_bytes=64)
+        k_scales = sb.tile([P, T], U8, name="k_scales", align_bytes=64)
+        old_sb = sb.tile([P, T], F32, name="old_sb")
+        mix_sb = sb.tile([P, 1], F32, name="mix_sb")
+        fade_sb = sb.tile([P, 1], F32, name="fade_sb")
+        placed = sb.tile([P, T], F32, name="placed")
+
+        nc.vector.memset(k_scales[:].bitcast(U32), 0)
+        nc.sync.dma_start(out=q1_raw[:], in_=query.rearrange("(p j) q -> p j q", j=PACK))
+        for quad in range(4):
+            nc.scalar.dma_start(
+                out=k_scales[32 * quad : 32 * quad + 4, :].bitcast(I32),
+                in_=keys_scales[0, 4 * quad : 4 * quad + 4, :].bitcast(I32),
+            )
+        nc.sync.dma_start(out=k_words[:].bitcast(I32), in_=keys_words[0].bitcast(I32))
+        nc.sync.dma_start(out=q2_raw[:], in_=query2.rearrange("(p j) q -> p j q", j=PACK))
+        nc.sync.dma_start(list1[:], offs)
+        nc.sync.dma_start(list2[:], offs2)
+        nc.sync.dma_start(out=old_sb[:], in_=old)
+        nc.gpsimd.dma_start(out=mix_sb[:], in_=mix)
+        nc.gpsimd.dma_start(out=fade_sb[:], in_=fade)
+        nc.vector.memset(placed[:], 0.0)
+
+        own_share = sb.tile([P, 1], F32, name="own_share")
+        run_share = sb.tile([P, 1], F32, name="run_share")
+        nc.gpsimd.tensor_scalar(own_share[:], mix_sb[:], -256.0, 256.0, ALU.mult, ALU.add)
+        nc.gpsimd.tensor_scalar(run_share[:], mix_sb[:], 256.0 / RUN, 0.0, ALU.mult, ALU.add)
+
+        q1_bf = sb.tile([P, Q, PACK], BF16, name="q1_bf", align_bytes=64)
+        q2_bf = sb.tile([P, Q, PACK], BF16, name="q2_bf", align_bytes=64)
+        q1_codes = sb.tile([P, Q], U32, name="q1_codes", align_bytes=64)
+        q2_codes = sb.tile([P, Q], U32, name="q2_codes", align_bytes=64)
+        q1_scales = sb.tile([P, Q], U8, name="q1_scales", align_bytes=64)
+        q2_scales = sb.tile([P, Q], U8, name="q2_scales", align_bytes=64)
+        nc.vector.tensor_copy(
+            out=q1_bf[:].rearrange("p (c i) j -> p c j i", i=4),
+            in_=q1_raw[:].rearrange("p j (c i) -> p c j i", i=4),
+        )
+        nc.vector.quantize_mx(
+            out=q1_codes[:].bitcast(FP8X4), scales=q1_scales[:], in_=q1_bf[:].rearrange("p q j -> p (q j)")
+        )
+        nc.scalar.copy(out=q2_bf[:], in_=q2_raw[:].rearrange("p j q -> p q j"))
+        nc.vector.quantize_mx(
+            out=q2_codes[:].bitcast(FP8X4), scales=q2_scales[:], in_=q2_bf[:].rearrange("p q j -> p (q j)")
+        )
+
+        a_sb = sb.tile([P, T], F32, name="a_sb")
+        b_sb = sb.tile([P, T], F32, name="b_sb")
+        for name, codes, scales, whole in (("a", q1_codes, q1_scales, a_sb), ("b", q2_codes, q2_scales, b_sb)):
+            for c0 in range(0, T, PIECE):
+                bank = ps.tile([P, PIECE], F32, name="bank_%s%d" % (name, c0))
+                nc.tensor.matmul_mx(
+                    out=bank[:],
+                    lhsT=codes[:].bitcast(FP8X4),
+                    lhsT_scale=scales[:],
+                    rhs=k_words[:, 2 * c0 : 2 * (c0 + PIECE)].bitcast(FP4X4),
+                    rhs_scale=k_scales[:, c0 : c0 + PIECE],
+                    start=True,
+                    stop=True,
+                )
+                if name == "a":
+                    nc.scalar.copy(out=whole[:, c0 : c0 + PIECE], in_=bank[:])
+                else:
+                    nc.vector.tensor_copy(out=whole[:, c0 : c0 + PIECE], in_=bank[:])
+
+        a1 = sb.tile([P, SLOTS], F32, name="a1")
+        a2 = sb.tile([P, SLOTS], F32, name="a2")
+        b1_hi = sb.tile([P, HALF], F32, name="b1_hi")
+        nc.scalar.activation(a1[:], a_sb[:].indirect(list1[:]), ACT.Copy)
+        nc.scalar.activation(a2[:], a_sb[:].indirect(list2[:]), ACT.Copy)
+        nc.scalar.activation(b1_hi[:], b_sb[:].indirect(list1[:, HALF_COLS:]), ACT.Copy)
+
+        left = sb.tile([P, SLOTS], F32, name="left")
+        right = sb.tile([P, SLOTS], F32, name="right")
+        score = sb.tile([P, SLOTS], F32, name="score")
+        nc.vector.tensor_tensor(left[:], b_sb[:].indirect(list2[:]), a1[:], ALU.mult)
+        nc.vector.tensor_tensor(right[:, :HALF], b_sb[:].indirect(list1[:, :HALF_COLS]), a2[:, :HALF], ALU.mult)
+        nc.vector.tensor_tensor(right[:, HALF:], b1_hi[:], a2[:, HALF:], ALU.mult)
+        halves = (slice(0, HALF), slice(HALF, SLOTS))
+        for h in halves:
+            nc.vector.tensor_tensor(score[:, h], left[:, h], right[:, h], ALU.subtract)
+        neg_max = sb.tile([P, 1], F32, name="neg_max")
+        nc.vector.tensor_reduce(neg_max[:], score[:], AX.X, ALU.max, negate=True)
+
+        sums = sb.tile([P, 2], F32, name="sums")
+        p = [sb.tile([P, HALF], F32, name="p%d" % i) for i in range(2)]
+        run_sum = [sb.tile([P, HALF // RUN], F32, name="run_sum%d" % i) for i in range(2)]
+        own = [sb.tile([P, HALF], F32, name="own%d" % i, tag="own%d" % i) for i in range(2)]
+        shared = [sb.tile([P, HALF], F32, name="shared%d" % i) for i in range(2)]
+        for i, h in enumerate(halves):
+            nc.scalar.activation(p[i][:], score[:, h], ACT.Exp, bias=neg_max[:], accum_out=sums[:, i : i + 1])
+            nc.vector.tensor_reduce(run_sum[i][:], p[i][:].rearrange("p (g r) -> p g r", r=RUN), AX.X, ALU.add)
+        for i in range(2):
+            nc.scalar.activation(own[i][:], p[i][:], ACT.Copy, scale=own_share[:])
+            nc.scalar.activation(
+                shared[i][:].rearrange("p (g r) -> p g r", r=RUN),
+                run_sum[i][:].unsqueeze(2).to_broadcast([P, HALF // RUN, RUN]),
+                ACT.Copy,
+                scale=run_share[:],
+            )
+        total = sb.tile([P, 1], F32, name="total")
+        inv_total = sb.tile([P, 1], F32, name="inv_total")
+        nc.vector.tensor_tensor(total[:], sums[:, 0:1], sums[:, 1:2], ALU.add)
+        nc.vector.reciprocal(inv_total[:], total[:])
+        for i in range(2):
+            cols = slice(i * HALF_COLS, (i + 1) * HALF_COLS)
+            nc.vector.tensor_tensor(placed[:].indirect(list1[:, cols]), own[i][:], shared[i][:], ALU.add)
+
+        faded = sb.tile([P, T], F32, name="faded", tag="own0")
+        nc.scalar.activation(faded[:], old_sb[:], ACT.Copy, scale=fade_sb[:])
+        for n, c0 in enumerate(range(0, T, STORE)):
+            cols = slice(c0, c0 + STORE)
+            result = sb.tile([P, STORE], F32, name="result%d" % n)
+            nc.vector.scalar_tensor_tensor(
+                result[:], placed[:, cols], inv_total[:], faded[:, cols], ALU.mult, ALU.add
+            )
+            queue = nc.sync if n % 2 == 0 else nc.scalar
+            queue.dma_start(out=out[:, cols], in_=result[:])

@@ -19,11 +19,12 @@ AX = mybir.AxisListType
 
 P = 128
 PACK = 4
-PIECE = 256
 HALF = SLOTS // 2
+QUARTER = SLOTS // 4
 LIST_COLS = SLOTS // 16
 HALF_COLS = LIST_COLS // 2
 STORE = 256
+PIECES = ((0, 256), (256, 256), (512, 256), (768, 128), (896, 128))
 
 
 def tile_attend_wedge_smoothpage_counts_heads_kernel(
@@ -45,7 +46,6 @@ def tile_attend_wedge_smoothpage_counts_heads_kernel(
         fade_sb = sb.tile([P, 1], F32, name="fade_sb")
         placed = sb.tile([P, T], F32, name="placed")
 
-        nc.vector.memset(k_scales[:].bitcast(U32), 0)
         nc.sync.dma_start(out=q1_raw[:], in_=query.rearrange("(p j) q -> p j q", j=PACK))
         for quad in range(4):
             nc.scalar.dma_start(
@@ -56,15 +56,10 @@ def tile_attend_wedge_smoothpage_counts_heads_kernel(
         nc.sync.dma_start(out=q2_raw[:], in_=query2.rearrange("(p j) q -> p j q", j=PACK))
         nc.sync.dma_start(list1[:], offs)
         nc.sync.dma_start(list2[:], offs2)
+        nc.sync.dma_start(out=mix_sb[:], in_=mix)
+        nc.sync.dma_start(out=fade_sb[:], in_=fade)
         nc.sync.dma_start(out=old_sb[:], in_=old)
-        nc.gpsimd.dma_start(out=mix_sb[:], in_=mix)
-        nc.gpsimd.dma_start(out=fade_sb[:], in_=fade)
         nc.vector.memset(placed[:], 0.0)
-
-        own_share = sb.tile([P, 1], F32, name="own_share")
-        run_share = sb.tile([P, 1], F32, name="run_share")
-        nc.gpsimd.tensor_scalar(own_share[:], mix_sb[:], -256.0, 256.0, ALU.mult, ALU.add)
-        nc.gpsimd.tensor_scalar(run_share[:], mix_sb[:], 256.0 / RUN, 0.0, ALU.mult, ALU.add)
 
         q1_bf = sb.tile([P, Q, PACK], BF16, name="q1_bf", align_bytes=64)
         q2_bf = sb.tile([P, Q, PACK], BF16, name="q2_bf", align_bytes=64)
@@ -79,74 +74,117 @@ def tile_attend_wedge_smoothpage_counts_heads_kernel(
         nc.vector.quantize_mx(
             out=q1_codes[:].bitcast(FP8X4), scales=q1_scales[:], in_=q1_bf[:].rearrange("p q j -> p (q j)")
         )
-        nc.scalar.copy(out=q2_bf[:], in_=q2_raw[:].rearrange("p j q -> p q j"))
+        nc.vector.tensor_copy(
+            out=q2_bf[:].rearrange("p (c i) j -> p c j i", i=4),
+            in_=q2_raw[:].rearrange("p j (c i) -> p c j i", i=4),
+        )
         nc.vector.quantize_mx(
             out=q2_codes[:].bitcast(FP8X4), scales=q2_scales[:], in_=q2_bf[:].rearrange("p q j -> p (q j)")
         )
 
         a_sb = sb.tile([P, T], F32, name="a_sb")
-        b_sb = sb.tile([P, T], F32, name="b_sb")
+        b_sb = sb.tile([P, T], F32, name="b_sb", tag="b_sb")
         for name, codes, scales, whole in (("a", q1_codes, q1_scales, a_sb), ("b", q2_codes, q2_scales, b_sb)):
-            for c0 in range(0, T, PIECE):
-                bank = ps.tile([P, PIECE], F32, name="bank_%s%d" % (name, c0))
+            for n, (c0, width) in enumerate(PIECES):
+                bank = ps.tile([P, width], F32, name="bank", tag="bank", bufs=8)
                 nc.tensor.matmul_mx(
                     out=bank[:],
                     lhsT=codes[:].bitcast(FP8X4),
                     lhsT_scale=scales[:],
-                    rhs=k_words[:, 2 * c0 : 2 * (c0 + PIECE)].bitcast(FP4X4),
-                    rhs_scale=k_scales[:, c0 : c0 + PIECE],
+                    rhs=k_words[:, 2 * c0 : 2 * (c0 + width)].bitcast(FP4X4),
+                    rhs_scale=k_scales[:, c0 : c0 + width],
                     start=True,
                     stop=True,
                 )
-                if name == "a":
-                    nc.scalar.copy(out=whole[:, c0 : c0 + PIECE], in_=bank[:])
+                if name == "a" and n in (2, 4):
+                    nc.vector.tensor_copy(out=whole[:, c0 : c0 + width], in_=bank[:])
                 else:
-                    nc.vector.tensor_copy(out=whole[:, c0 : c0 + PIECE], in_=bank[:])
+                    nc.scalar.copy(out=whole[:, c0 : c0 + width], in_=bank[:])
 
+        lo, hi = slice(0, HALF), slice(HALF, SLOTS)
+        lo_cols, hi_cols = slice(0, HALF_COLS), slice(HALF_COLS, LIST_COLS)
         a1 = sb.tile([P, SLOTS], F32, name="a1")
-        a2 = sb.tile([P, SLOTS], F32, name="a2")
-        b1_hi = sb.tile([P, HALF], F32, name="b1_hi")
-        nc.scalar.activation(a1[:], a_sb[:].indirect(list1[:]), ACT.Copy)
-        nc.scalar.activation(a2[:], a_sb[:].indirect(list2[:]), ACT.Copy)
-        nc.scalar.activation(b1_hi[:], b_sb[:].indirect(list1[:, HALF_COLS:]), ACT.Copy)
+        b1 = sb.tile([P, SLOTS], F32, name="b1")
+        b2_hi = sb.tile([P, HALF], F32, name="b2_hi")
+        nc.vector.tensor_copy(a1[:, lo], a_sb[:].indirect(list1[:, lo_cols]))
+        nc.vector.tensor_copy(a1[:, hi], a_sb[:].indirect(list1[:, hi_cols]))
+        nc.scalar.activation(b1[:, lo], b_sb[:].indirect(list1[:, lo_cols]), ACT.Copy)
+        nc.scalar.activation(b1[:, hi], b_sb[:].indirect(list1[:, hi_cols]), ACT.Copy)
+        nc.scalar.activation(b2_hi[:], b_sb[:].indirect(list2[:, hi_cols]), ACT.Copy)
 
         left = sb.tile([P, SLOTS], F32, name="left")
         right = sb.tile([P, SLOTS], F32, name="right")
         score = sb.tile([P, SLOTS], F32, name="score")
-        nc.vector.tensor_tensor(left[:], b_sb[:].indirect(list2[:]), a1[:], ALU.mult)
-        nc.vector.tensor_tensor(right[:, :HALF], b_sb[:].indirect(list1[:, :HALF_COLS]), a2[:, :HALF], ALU.mult)
-        nc.vector.tensor_tensor(right[:, HALF:], b1_hi[:], a2[:, HALF:], ALU.mult)
-        halves = (slice(0, HALF), slice(HALF, SLOTS))
-        for h in halves:
-            nc.vector.tensor_tensor(score[:, h], left[:, h], right[:, h], ALU.subtract)
+        neg_max_lo = sb.tile([P, 1], F32, name="neg_max_lo")
         neg_max = sb.tile([P, 1], F32, name="neg_max")
-        nc.vector.tensor_reduce(neg_max[:], score[:], AX.X, ALU.max, negate=True)
+        neg_score_hi = sb.tile([P, HALF], F32, name="neg_score_hi")
+        nc.vector.tensor_tensor(left[:, lo], b_sb[:].indirect(list2[:, lo_cols]), a1[:, lo], ALU.mult)
+        nc.vector.tensor_tensor(right[:, lo], a_sb[:].indirect(list2[:, lo_cols]), b1[:, lo], ALU.mult)
+        nc.vector.tensor_tensor(score[:, lo], left[:, lo], right[:, lo], ALU.subtract)
+        nc.vector.tensor_tensor(right[:, hi], a_sb[:].indirect(list2[:, hi_cols]), b1[:, hi], ALU.mult)
+        nc.vector.tensor_reduce(neg_max_lo[:], score[:, lo], AX.X, ALU.max, negate=True)
+        nc.vector.tensor_tensor(left[:, hi], b2_hi[:], a1[:, hi], ALU.mult)
+        nc.vector.tensor_tensor(score[:, hi], left[:, hi], right[:, hi], ALU.subtract)
+        nc.vector.tensor_scalar(
+            neg_score_hi[:], score[:, hi], -1.0, neg_max_lo[:], ALU.mult, ALU.min, accum_out=neg_max[:]
+        )
 
-        sums = sb.tile([P, 2], F32, name="sums")
-        p = [sb.tile([P, HALF], F32, name="p%d" % i) for i in range(2)]
-        run_sum = [sb.tile([P, HALF // RUN], F32, name="run_sum%d" % i) for i in range(2)]
-        own = [sb.tile([P, HALF], F32, name="own%d" % i, tag="own%d" % i) for i in range(2)]
-        shared = [sb.tile([P, HALF], F32, name="shared%d" % i) for i in range(2)]
-        for i, h in enumerate(halves):
-            nc.scalar.activation(p[i][:], score[:, h], ACT.Exp, bias=neg_max[:], accum_out=sums[:, i : i + 1])
-            nc.vector.tensor_reduce(run_sum[i][:], p[i][:].rearrange("p (g r) -> p g r", r=RUN), AX.X, ALU.add)
-        for i in range(2):
-            nc.scalar.activation(own[i][:], p[i][:], ACT.Copy, scale=own_share[:])
-            nc.scalar.activation(
-                shared[i][:].rearrange("p (g r) -> p g r", r=RUN),
-                run_sum[i][:].unsqueeze(2).to_broadcast([P, HALF // RUN, RUN]),
-                ACT.Copy,
-                scale=run_share[:],
-            )
+        shares = sb.tile([P, 2], F32, name="shares", tag="b_sb")
+        own_share, run_share = shares[:, 0:1], shares[:, 1:2]
+        nc.scalar.activation(own_share, mix_sb[:], ACT.Copy, bias=256.0, scale=-256.0)
+        nc.scalar.activation(run_share, mix_sb[:], ACT.Copy, scale=256.0 / RUN)
+
+        runs = HALF // RUN
+        p_lo = sb.tile([P, HALF], F32, name="p_lo")
+        p_hi = sb.tile([P, HALF], F32, name="p_hi")
+        sum_lo = sb.tile([P, 1], F32, name="sum_lo")
+        sum_hi = sb.tile([P, 1], F32, name="sum_hi")
+        run_lo = sb.tile([P, runs], F32, name="run_lo")
+        run_hi = sb.tile([P, runs], F32, name="run_hi")
+        own_lo = sb.tile([P, HALF], F32, name="own_lo")
+        own_hi = sb.tile([P, HALF], F32, name="own_hi")
+        mixed_lo = sb.tile([P, HALF], F32, name="mixed_lo")
+        shared_hi = sb.tile([P, HALF], F32, name="shared_hi")
+        rebase = [sb.tile([P, QUARTER], F32, name="rebase%d" % i, tag="rebase%d" % i) for i in range(2)]
+
+        nc.scalar.activation(p_lo[:], score[:, lo], ACT.Exp, bias=neg_max_lo[:], accum_out=sum_lo[:])
+        nc.scalar.activation(own_lo[:], p_lo[:], ACT.Copy, scale=own_share)
+        nc.vector.tensor_reduce(run_lo[:], p_lo[:].rearrange("p (g r) -> p g r", r=RUN), AX.X, ALU.add)
+        nc.vector.scalar_tensor_tensor(
+            mixed_lo[:].rearrange("p (g r) -> p g r", r=RUN),
+            run_lo[:].unsqueeze(2).to_broadcast([P, runs, RUN]),
+            run_share,
+            own_lo[:].rearrange("p (g r) -> p g r", r=RUN),
+            ALU.mult,
+            ALU.add,
+        )
+        spread_max = neg_max_lo[:].to_broadcast([P, QUARTER])
+        nc.scalar.activation(rebase[0][:], spread_max, ACT.Exp, bias=neg_max[:], scale=-1.0)
+        nc.scalar.activation(p_hi[:], neg_score_hi[:], ACT.Exp, bias=neg_max[:], scale=-1.0, accum_out=sum_hi[:])
+        nc.scalar.activation(rebase[1][:], spread_max, ACT.Exp, bias=neg_max[:], scale=-1.0)
+        nc.scalar.activation(own_hi[:], p_hi[:], ACT.Copy, scale=own_share)
+
+        quarter_cols = HALF_COLS // 2
+        nc.vector.tensor_tensor(
+            placed[:].indirect(list1[:, :quarter_cols]), mixed_lo[:, :QUARTER], rebase[0][:], ALU.mult
+        )
+        nc.vector.tensor_reduce(run_hi[:], p_hi[:].rearrange("p (g r) -> p g r", r=RUN), AX.X, ALU.add)
         total = sb.tile([P, 1], F32, name="total")
         inv_total = sb.tile([P, 1], F32, name="inv_total")
-        nc.vector.tensor_tensor(total[:], sums[:, 0:1], sums[:, 1:2], ALU.add)
+        nc.vector.scalar_tensor_tensor(total[:], sum_lo[:], rebase[1][:, 0:1], sum_hi[:], ALU.mult, ALU.add)
+        nc.vector.tensor_tensor(
+            placed[:].indirect(list1[:, quarter_cols:HALF_COLS]), mixed_lo[:, QUARTER:], rebase[1][:], ALU.mult
+        )
         nc.vector.reciprocal(inv_total[:], total[:])
-        for i in range(2):
-            cols = slice(i * HALF_COLS, (i + 1) * HALF_COLS)
-            nc.vector.tensor_tensor(placed[:].indirect(list1[:, cols]), own[i][:], shared[i][:], ALU.add)
+        nc.scalar.activation(
+            shared_hi[:].rearrange("p (g r) -> p g r", r=RUN),
+            run_hi[:].unsqueeze(2).to_broadcast([P, runs, RUN]),
+            ACT.Copy,
+            scale=run_share,
+        )
+        nc.vector.tensor_tensor(placed[:].indirect(list1[:, hi_cols]), own_hi[:], shared_hi[:], ALU.add)
 
-        faded = sb.tile([P, T], F32, name="faded", tag="own0")
+        faded = sb.tile([P, T], F32, name="faded", tag="rebase1")
         nc.scalar.activation(faded[:], old_sb[:], ACT.Copy, scale=fade_sb[:])
         for n, c0 in enumerate(range(0, T, STORE)):
             cols = slice(c0, c0 + STORE)

@@ -48,7 +48,7 @@ def tile_attend_wedge_smoothpage_counts_heads_kernel(
 
         nc.sync.dma_start(out=q1_raw[:], in_=query.rearrange("(p j) q -> p j q", j=PACK))
         for quad in range(4):
-            nc.scalar.dma_start(
+            nc.sync.dma_start(
                 out=k_scales[32 * quad : 32 * quad + 4, :].bitcast(I32),
                 in_=keys_scales[0, 4 * quad : 4 * quad + 4, :].bitcast(I32),
             )
@@ -84,8 +84,8 @@ def tile_attend_wedge_smoothpage_counts_heads_kernel(
 
         a_sb = sb.tile([P, T], F32, name="a_sb")
         b_sb = sb.tile([P, T], F32, name="b_sb", tag="b_sb")
-        for name, codes, scales, whole in (("a", q1_codes, q1_scales, a_sb), ("b", q2_codes, q2_scales, b_sb)):
-            for n, (c0, width) in enumerate(PIECES):
+        for codes, scales, whole in ((q1_codes, q1_scales, a_sb), (q2_codes, q2_scales, b_sb)):
+            for c0, width in PIECES:
                 bank = ps.tile([P, width], F32, name="bank", tag="bank", bufs=8)
                 nc.tensor.matmul_mx(
                     out=bank[:],
@@ -96,10 +96,7 @@ def tile_attend_wedge_smoothpage_counts_heads_kernel(
                     start=True,
                     stop=True,
                 )
-                if name == "a" and n in (2, 4):
-                    nc.vector.tensor_copy(out=whole[:, c0 : c0 + width], in_=bank[:])
-                else:
-                    nc.scalar.copy(out=whole[:, c0 : c0 + width], in_=bank[:])
+                nc.scalar.copy(out=whole[:, c0 : c0 + width], in_=bank[:])
 
         lo, hi = slice(0, HALF), slice(HALF, SLOTS)
         lo_cols, hi_cols = slice(0, HALF_COLS), slice(HALF_COLS, LIST_COLS)

from contextlib import ExitStack

import concourse.mybir as mybir

D, T, SLOTS, Q, RUN = 512, 1024, 512, 128, 8
FLOPS = 2 * 2 * D * Q * T

F32 = mybir.dt.float32
BF16 = mybir.dt.bfloat16
I32 = mybir.dt.int32
U32 = mybir.dt.uint32
U16 = mybir.dt.uint16
U8 = mybir.dt.uint8
FP8X4 = mybir.dt.float8_e4m3fn_x4
FP4X4 = mybir.dt.float4_e2m1fn_x4
ALU = mybir.AluOpType
ACT = mybir.ActivationFunctionType
AX = mybir.AxisListType

P = 128
PACK = 4
HALF = SLOTS // 2
QUARTER = SLOTS // 4
LIST_COLS = SLOTS // 16
HALF_COLS = LIST_COLS // 2
STORE = 256
PIECES = ((0, 256), (256, 256), (512, 256), (768, 128), (896, 128))


def tile_attend_wedge_smoothpage_counts_heads_kernel(
    tc, query, query2, keys_words, keys_scales, mix, old, fade, offs, offs2, out
):
    nc = tc.nc
    with ExitStack() as ctx:
        sb = ctx.enter_context(tc.tile_pool(name="sb", bufs=1))
        ps = ctx.enter_context(tc.psum_pool(name="ps", bufs=1))

        list1 = sb.tile([P, LIST_COLS], U16, name="list1")
        list2 = sb.tile([P, LIST_COLS], U16, name="list2")
        q1_raw = sb.tile([P, PACK, Q], F32, name="q1_raw")
        q2_raw = sb.tile([P, PACK, Q], F32, name="q2_raw")
        k_words = sb.tile([P, 2 * T], U8, name="k_words", align_bytes=64)
        k_scales = sb.tile([P, T], U8, name="k_scales", align_bytes=64)
        old_sb = sb.tile([P, T], F32, name="old_sb")
        mix_sb = sb.tile([P, 1], F32, name="mix_sb")
        fade_sb = sb.tile([P, 1], F32, name="fade_sb")
        placed = sb.tile([P, T], F32, name="placed")

        nc.sync.dma_start(out=q1_raw[:], in_=query.rearrange("(p j) q -> p j q", j=PACK))
        for quad in range(4):
            nc.sync.dma_start(
                out=k_scales[32 * quad : 32 * quad + 4, :].bitcast(I32),
                in_=keys_scales[0, 4 * quad : 4 * quad + 4, :].bitcast(I32),
            )
        nc.sync.dma_start(out=k_words[:].bitcast(I32), in_=keys_words[0].bitcast(I32))
        nc.sync.dma_start(out=q2_raw[:], in_=query2.rearrange("(p j) q -> p j q", j=PACK))
        nc.sync.dma_start(list1[:], offs)
        nc.sync.dma_start(list2[:], offs2)
        nc.sync.dma_start(out=mix_sb[:], in_=mix)
        nc.sync.dma_start(out=fade_sb[:], in_=fade)
        nc.sync.dma_start(out=old_sb[:], in_=old)
        nc.vector.memset(placed[:], 0.0)

        q1_bf = sb.tile([P, Q, PACK], BF16, name="q1_bf", align_bytes=64)
        q2_bf = sb.tile([P, Q, PACK], BF16, name="q2_bf", align_bytes=64)
        q1_codes = sb.tile([P, Q], U32, name="q1_codes", align_bytes=64)
        q2_codes = sb.tile([P, Q], U32, name="q2_codes", align_bytes=64)
        q1_scales = sb.tile([P, Q], U8, name="q1_scales", align_bytes=64)
        q2_scales = sb.tile([P, Q], U8, name="q2_scales", align_bytes=64)
        nc.vector.tensor_copy(
            out=q1_bf[:].rearrange("p (c i) j -> p c j i", i=4),
            in_=q1_raw[:].rearrange("p j (c i) -> p c j i", i=4),
        )
        nc.vector.quantize_mx(
            out=q1_codes[:].bitcast(FP8X4), scales=q1_scales[:], in_=q1_bf[:].rearrange("p q j -> p (q j)")
        )
        nc.vector.tensor_copy(
            out=q2_bf[:].rearrange("p (c i) j -> p c j i", i=4),
            in_=q2_raw[:].rearrange("p j (c i) -> p c j i", i=4),
        )
        nc.vector.quantize_mx(
            out=q2_codes[:].bitcast(FP8X4), scales=q2_scales[:], in_=q2_bf[:].rearrange("p q j -> p (q j)")
        )

        a_sb = sb.tile([P, T], F32, name="a_sb")
        b_sb = sb.tile([P, T], F32, name="b_sb", tag="b_sb")
        for codes, scales, whole in ((q1_codes, q1_scales, a_sb), (q2_codes, q2_scales, b_sb)):
            for c0, width in PIECES:
                bank = ps.tile([P, width], F32, name="bank", tag="bank", bufs=8)
                nc.tensor.matmul_mx(
                    out=bank[:],
                    lhsT=codes[:].bitcast(FP8X4),
                    lhsT_scale=scales[:],
                    rhs=k_words[:, 2 * c0 : 2 * (c0 + width)].bitcast(FP4X4),
                    rhs_scale=k_scales[:, c0 : c0 + width],
                    start=True,
                    stop=True,
                )
                nc.scalar.copy(out=whole[:, c0 : c0 + width], in_=bank[:])

        lo, hi = slice(0, HALF), slice(HALF, SLOTS)
        lo_cols, hi_cols = slice(0, HALF_COLS), slice(HALF_COLS, LIST_COLS)
        a1 = sb.tile([P, SLOTS], F32, name="a1")
        b1 = sb.tile([P, SLOTS], F32, name="b1")
        b2_hi = sb.tile([P, HALF], F32, name="b2_hi")
        nc.vector.tensor_copy(a1[:, lo], a_sb[:].indirect(list1[:, lo_cols]))
        nc.vector.tensor_copy(a1[:, hi], a_sb[:].indirect(list1[:, hi_cols]))
        nc.scalar.activation(b1[:, lo], b_sb[:].indirect(list1[:, lo_cols]), ACT.Copy)
        nc.scalar.activation(b1[:, hi], b_sb[:].indirect(list1[:, hi_cols]), ACT.Copy)
        nc.scalar.activation(b2_hi[:], b_sb[:].indirect(list2[:, hi_cols]), ACT.Copy)

        left = sb.tile([P, SLOTS], F32, name="left")
        right = sb.tile([P, SLOTS], F32, name="right")
        score = sb.tile([P, SLOTS], F32, name="score")
        neg_max_lo = sb.tile([P, 1], F32, name="neg_max_lo")
        neg_max = sb.tile([P, 1], F32, name="neg_max")
        neg_score_hi = sb.tile([P, HALF], F32, name="neg_score_hi")
        nc.vector.tensor_tensor(left[:, lo], b_sb[:].indirect(list2[:, lo_cols]), a1[:, lo], ALU.mult)
        nc.vector.tensor_tensor(right[:, lo], a_sb[:].indirect(list2[:, lo_cols]), b1[:, lo], ALU.mult)
        nc.vector.tensor_tensor(score[:, lo], left[:, lo], right[:, lo], ALU.subtract)
        nc.vector.tensor_tensor(right[:, hi], a_sb[:].indirect(list2[:, hi_cols]), b1[:, hi], ALU.mult)
        nc.vector.tensor_reduce(neg_max_lo[:], score[:, lo], AX.X, ALU.max, negate=True)
        nc.vector.tensor_tensor(left[:, hi], b2_hi[:], a1[:, hi], ALU.mult)
        nc.vector.tensor_tensor(score[:, hi], left[:, hi], right[:, hi], ALU.subtract)
        nc.vector.tensor_scalar(
            neg_score_hi[:], score[:, hi], -1.0, neg_max_lo[:], ALU.mult, ALU.min, accum_out=neg_max[:]
        )

        shares = sb.tile([P, 2], F32, name="shares", tag="b_sb")
        own_share, run_share = shares[:, 0:1], shares[:, 1:2]
        nc.scalar.activation(own_share, mix_sb[:], ACT.Copy, bias=256.0, scale=-256.0)
        nc.scalar.activation(run_share, mix_sb[:], ACT.Copy, scale=256.0 / RUN)

        runs = HALF // RUN
        p_lo = sb.tile([P, HALF], F32, name="p_lo")
        p_hi = sb.tile([P, HALF], F32, name="p_hi")
        sum_lo = sb.tile([P, 1], F32, name="sum_lo")
        sum_hi = sb.tile([P, 1], F32, name="sum_hi")
        run_lo = sb.tile([P, runs], F32, name="run_lo")
        run_hi = sb.tile([P, runs], F32, name="run_hi")
        own_lo = sb.tile([P, HALF], F32, name="own_lo")
        own_hi = sb.tile([P, HALF], F32, name="own_hi")
        mixed_lo = sb.tile([P, HALF], F32, name="mixed_lo")
        shared_hi = sb.tile([P, HALF], F32, name="shared_hi")
        rebase = [sb.tile([P, QUARTER], F32, name="rebase%d" % i, tag="rebase%d" % i) for i in range(2)]

        nc.scalar.activation(p_lo[:], score[:, lo], ACT.Exp, bias=neg_max_lo[:], accum_out=sum_lo[:])
        nc.scalar.activation(own_lo[:], p_lo[:], ACT.Copy, scale=own_share)
        nc.vector.tensor_reduce(run_lo[:], p_lo[:].rearrange("p (g r) -> p g r", r=RUN), AX.X, ALU.add)
        nc.vector.scalar_tensor_tensor(
            mixed_lo[:].rearrange("p (g r) -> p g r", r=RUN),
            run_lo[:].unsqueeze(2).to_broadcast([P, runs, RUN]),
            run_share,
            own_lo[:].rearrange("p (g r) -> p g r", r=RUN),
            ALU.mult,
            ALU.add,
        )
        spread_max = neg_max_lo[:].to_broadcast([P, QUARTER])
        nc.scalar.activation(rebase[0][:], spread_max, ACT.Exp, bias=neg_max[:], scale=-1.0)
        nc.scalar.activation(p_hi[:], neg_score_hi[:], ACT.Exp, bias=neg_max[:], scale=-1.0, accum_out=sum_hi[:])
        nc.scalar.activation(rebase[1][:], spread_max, ACT.Exp, bias=neg_max[:], scale=-1.0)
        nc.scalar.activation(own_hi[:], p_hi[:], ACT.Copy, scale=own_share)

        quarter_cols = HALF_COLS // 2
        nc.vector.tensor_tensor(
            placed[:].indirect(list1[:, :quarter_cols]), mixed_lo[:, :QUARTER], rebase[0][:], ALU.mult
        )
        nc.vector.tensor_reduce(run_hi[:], p_hi[:].rearrange("p (g r) -> p g r", r=RUN), AX.X, ALU.add)
        total = sb.tile([P, 1], F32, name="total")
        inv_total = sb.tile([P, 1], F32, name="inv_total")
        nc.vector.scalar_tensor_tensor(total[:], sum_lo[:], rebase[1][:, 0:1], sum_hi[:], ALU.mult, ALU.add)
        nc.vector.tensor_tensor(
            placed[:].indirect(list1[:, quarter_cols:HALF_COLS]), mixed_lo[:, QUARTER:], rebase[1][:], ALU.mult
        )
        nc.vector.reciprocal(inv_total[:], total[:])
        nc.scalar.activation(
            shared_hi[:].rearrange("p (g r) -> p g r", r=RUN),
            run_hi[:].unsqueeze(2).to_broadcast([P, runs, RUN]),
            ACT.Copy,
            scale=run_share,
        )
        nc.vector.tensor_tensor(placed[:].indirect(list1[:, hi_cols]), own_hi[:], shared_hi[:], ALU.add)

        faded = sb.tile([P, T], F32, name="faded", tag="rebase1")
        nc.scalar.activation(faded[:], old_sb[:], ACT.Copy, scale=fade_sb[:])
        for n, c0 in enumerate(range(0, T, STORE)):
            cols = slice(c0, c0 + STORE)
            result = sb.tile([P, STORE], F32, name="result%d" % n)
            nc.vector.scalar_tensor_tensor(
                result[:], placed[:, cols], inv_total[:], faded[:, cols], ALU.mult, ALU.add
            )
            queue = nc.sync if n % 2 == 0 else nc.scalar
            queue.dma_start(out=out[:, cols], in_=result[:])
